import numpy as np
import ml_dtypes


def mxq(x, axis, fmt="e4m3"):
    dtype, down = {"e4m3": (ml_dtypes.float8_e4m3fn, 7), "e5m2": (ml_dtypes.float8_e5m2, 14)}[fmt]
    v = np.moveaxis(np.asarray(x, np.float32).astype(ml_dtypes.bfloat16).astype(np.float64), axis, -1)
    blocks = v.reshape(v.shape[:-1] + (-1, 32))
    amax = np.abs(blocks).max(-1, keepdims=True)
    byte = np.maximum(np.where(amax > 0, np.frexp(amax)[1] - 1 + 127, 0) - down, 1)
    scale = np.exp2(byte - 127.0)
    codes = (blocks / scale).astype(np.float32).astype(dtype).astype(np.float64)
    return np.moveaxis((codes * scale).reshape(v.shape), -1, axis)


WIDE = False


def mx_kscale(k):
    if not WIDE:
        return np.ones(k)
    levels = np.array([10, -10, 5, -5, 0])
    if k % 512:
        return np.exp2(np.random.permutation(np.resize(levels, k // 32))).repeat(32)
    a = np.empty((k // 512, 16))
    for p in range(k // 512):
        a[p, :8] = np.random.permutation(np.resize(levels, 8))
        for g in range(8):
            far = levels[np.abs(levels - a[p, g]) >= 10]
            a[p, g + 8] = far[np.random.randint(len(far))]
    return np.exp2(a.ravel()).repeat(32)


def f64(x):
    return np.asarray(x).astype(np.float64)


def striped8(idx):
    return np.concatenate([v.reshape(-1, 16).T for v in idx]).astype(np.uint16)


def unstriped8(offs):
    return np.stack([offs[16 * g:16 * g + 16].T.reshape(-1) for g in range(8)]).astype(np.int64)


E2M1 = np.array([0.0, 0.5, 1.0, 1.5, 2.0, 3.0, 4.0, 6.0, -0.0, -0.5, -1.0, -1.5, -2.0, -3.0, -4.0, -6.0])


def pack_weight(w, fmt):
    k, n = w.shape
    w = f64(np.asarray(w, np.float32).astype(ml_dtypes.bfloat16)).reshape(k // 32, 32, n)
    amax = np.abs(w).max(1)
    if fmt == "e4m3":
        byte = np.frexp(amax)[1] - 1 + 127 - 7
    else:
        mant, ex = np.frexp(amax / 6.0)
        byte = np.where(mant > 0.5, ex, ex - 1) + 127
    byte = np.clip(np.where(amax > 0, byte, 1), 1, 254)
    scaled = (w * np.exp2(127.0 - byte)[:, None, :]).reshape(k, n).astype(np.float32)
    by_word = np.ascontiguousarray(scaled.reshape(k // 512, 128, 4, n).transpose(0, 1, 3, 2))
    if fmt == "e4m3":
        words = by_word.astype(ml_dtypes.float8_e4m3fn).view(np.uint8)
    else:
        c = by_word.astype(ml_dtypes.float4_e2m1fn).view(np.uint8) & 0xF
        words = (c[..., 0::2] | (c[..., 1::2] << 4)).reshape(k // 512, 128, 2 * n)
    return np.ascontiguousarray(words), np.ascontiguousarray(byte.astype(np.uint8).reshape(k // 512, 16, n))


def unpack_weight(words, scales, fmt):
    g, _, n = scales.shape
    words = np.ascontiguousarray(words).reshape(g, 128, n, -1)
    if fmt == "e4m3":
        vals = words.view(ml_dtypes.float8_e4m3fn).astype(np.float64)
    else:
        nib = np.empty((g, 128, n, 4), np.uint8)
        nib[..., 0::2] = words & 0xF
        nib[..., 1::2] = words >> 4
        vals = E2M1[nib]
    vals = vals * np.repeat(np.exp2(scales.astype(np.float64) - 127.0), 8, axis=1)[..., None]
    return vals.transpose(0, 1, 3, 2).reshape(g * 512, n)


K, L, M, T, S = 512, 512, 1024, 2048, 512


def setup_inputs():
    n = np.random.standard_normal
    s1 = mx_kscale(K)[:, None]
    s2 = mx_kscale(L)[:, None]
    p_w4 = pack_weight(n((K, M)) / np.sqrt(K) / s1, "e2m1")
    return {
        "xT": (n((K, T)) * s1).astype(np.float32),
        "w4_words": p_w4[0],
        "w4_scales": p_w4[1],
        "c": (n((L, S)) * s2).astype(np.float32),
        "u": (n((L, M)) / np.sqrt(L) / s2).astype(np.float32),
        "wgt": np.repeat(np.random.uniform(0.5, 2.0, (8, S)), 16, axis=0).astype(np.float32),
        "b": (0.3 * n(1024)).astype(np.float32),
        "offs": striped8(np.stack([np.random.permutation(T)[:S] for _ in range(8)])),
    }


def reference(xT, w4_words, w4_scales, c, u, wgt, b, offs):
    idx = unstriped8(offs)
    group = np.arange(K) % 512 // 64
    xg = f64(wgt)[np.arange(K) // 4 % 128] * f64(xT)[np.arange(K)[:, None], idx[group]]
    xT_ = mxq(xg, 0, "e4m3")
    w4_ = unpack_weight(w4_words, w4_scales, "e2m1")
    c_ = mxq(f64(c), 0, "e4m3")
    u_ = mxq(f64(u), 0, "e4m3")
    y = w4_.T @ xT_ + u_.T @ c_
    return y + f64(b)[:, None]

@@ -1,0 +1,153 @@
+from contextlib import ExitStack
+
+import concourse.mybir as mybir
+from concourse.masks import make_identity
+
+F32 = mybir.dt.float32
+BF16 = mybir.dt.bfloat16
+I32 = mybir.dt.int32
+U32 = mybir.dt.uint32
+U16 = mybir.dt.uint16
+U8 = mybir.dt.uint8
+E4M3X4 = mybir.dt.float8_e4m3fn_x4
+E2M1X4 = mybir.dt.float4_e2m1fn_x4
+MULT = mybir.AluOpType.mult
+ADD = mybir.AluOpType.add
+IDENTITY = mybir.ActivationFunctionType.Identity
+
+P = 128
+PACK = 4
+K, L, M, T, S = 512, 512, 1024, 2048, 512
+NB = M // P
+U_WIDTHS = (512, 256, 256,)
+U_STARTS = (0, 512, 768,)
+U_SCALAR = (192, 128, 128,)
+C_SCALAR = 192
+G_CUTS = (0, 256, 512)
+XG_ON = "SV"
+DRAIN_ON = "VSSVSSVS"
+
+FLOPS = 2 * M * S * (K + L)
+
+
+def tile_list_hmix_bias_kernel(tc, xT, w4_words, w4_scales, c, u, wgt, b, offs, out):
+    nc = tc.nc
+    with ExitStack() as ctx:
+        keep = ctx.enter_context(tc.tile_pool(name="keep", bufs=1))
+        psum = ctx.enter_context(tc.psum_pool(name="psum", bufs=1))
+
+        offsets = keep.tile([P, S // 16], U16, name="offsets")
+        weights = keep.tile([P, S], F32, name="weights")
+        planes = [keep.tile([P, T], F32, name=f"plane{i}") for i in range(PACK)]
+        c_raw = keep.tile([P, PACK, S], F32, name="c_raw")
+        u_raw = [keep.tile([P, PACK, w], F32, name=f"u_raw{q}") for q, w in enumerate(U_WIDTHS)]
+        w4_t = keep.tile([P, 2 * M], U8, name="w4_t", align_bytes=64)
+        w4_s = keep.tile([P, M], U8, name="w4_s", align_bytes=64)
+        b_rows = keep.tile([P, P], F32, name="b_rows")
+        b_cols = keep.tile([P, NB], F32, name="b_cols")
+        ident = keep.tile([P, P], F32, name="ident")
+        warm = keep.tile([P, 1], F32, name="warm")
+
+        xv = xT.rearrange("(p j) t -> p j t", j=PACK)
+        cv = c.rearrange("(p j) s -> p j s", j=PACK)
+        uv = u.rearrange("(p j) n -> p j n", j=PACK)
+
+        nc.vector.memset(b_rows[:], 0.0)
+        nc.vector.memset(w4_s[:].bitcast(I32), 0)
+        make_identity(nc, ident[:])
+        nc.scalar.activation(warm[:], b_rows[:, 0:1], IDENTITY)
+
+        nc.sync.dma_start(offsets[:], offs)
+        nc.scalar.dma_start(b_rows[0:NB, :], b.rearrange("(t m) -> t m", m=P))
+        for q in range(4):
+            nc.scalar.dma_start(
+                w4_s[32 * q : 32 * q + 4, :].bitcast(I32), w4_scales[0, 4 * q : 4 * q + 4, :].bitcast(I32)
+            )
+        nc.sync.dma_start(planes[0][:], xv[:, 0, :])
+        nc.sync.dma_start(weights[:], wgt)
+        nc.sync.dma_start(planes[1][:], xv[:, 1, :])
+        nc.sync.dma_start(planes[2][:], xv[:, 2, :])
+        nc.sync.dma_start(planes[3][:], xv[:, 3, :])
+        nc.sync.dma_start(c_raw[:], cv)
+        nc.sync.dma_start(u_raw[0][:], uv[:, :, U_STARTS[0] : U_STARTS[0] + U_WIDTHS[0]])
+        nc.sync.dma_start(w4_t[:], w4_words[0])
+        nc.sync.dma_start(u_raw[1][:], uv[:, :, U_STARTS[1] : U_STARTS[1] + U_WIDTHS[1]])
+        nc.sync.dma_start(u_raw[2][:], uv[:, :, U_STARTS[2] : U_STARTS[2] + U_WIDTHS[2]])
+
+        b_ps = psum.tile([P, P], F32, name="b_ps", tag="acc7")
+        nc.tensor.transpose(b_ps[:], b_rows[:], ident[:])
+        nc.vector.tensor_copy(b_cols[:], b_ps[:, 0:NB])
+
+        c_bf = keep.tile([P, S, PACK], BF16, name="c_bf", align_bytes=64)
+        c_codes = keep.tile([P, S], U32, name="c_codes", align_bytes=64)
+        c_scales = keep.tile([P, S], U8, name="c_scales", align_bytes=64)
+        g = [keep.tile([P, PACK, hi - lo], F32, name=f"g{lo}") for lo, hi in zip(G_CUTS, G_CUTS[1:])]
+        u_bf = [keep.tile([P, w, PACK], BF16, name=f"u_bf{q}", align_bytes=64) for q, w in enumerate(U_WIDTHS)]
+        u_codes = [keep.tile([P, w], U32, name=f"u_codes{q}", align_bytes=64) for q, w in enumerate(U_WIDTHS)]
+        u_scales = [keep.tile([P, w], U8, name=f"u_scales{q}", align_bytes=64) for q, w in enumerate(U_WIDTHS)]
+        xg_bf = keep.tile([P, S, PACK], BF16, name="xg_bf", align_bytes=64)
+        xg_codes = keep.tile([P, S], U32, name="xg_codes", align_bytes=64)
+        xg_scales = keep.tile([P, S], U8, name="xg_scales", align_bytes=64)
+        res = [keep.tile([P, S], F32, name=f"res{n}") for n in range(NB)]
+
+        def lay(engine, dst, src):
+            (nc.scalar.copy if engine == "S" else nc.vector.tensor_copy)(dst, src.rearrange("p j w -> p w j"))
+
+        def quant(codes, scales, src):
+            nc.vector.quantize_mx(out=codes.bitcast(E4M3X4), scales=scales, in_=src.rearrange("p w j -> p (w j)"))
+
+        for i in range(PACK):
+            for h, (lo, hi) in enumerate(zip(G_CUTS, G_CUTS[1:])):
+                nc.vector.tensor_tensor(
+                    g[h][:, i, :], planes[i][:].indirect(offsets[:, lo // 16 : hi // 16]), weights[:, lo:hi], MULT
+                )
+        for h, (lo, hi) in enumerate(zip(G_CUTS, G_CUTS[1:])):
+            lay(XG_ON[h], xg_bf[:, lo:hi, :], g[h][:])
+
+        lay("S", c_bf[:, 0:C_SCALAR, :], c_raw[:, :, 0:C_SCALAR])
+        lay("V", c_bf[:, C_SCALAR:S, :], c_raw[:, :, C_SCALAR:S])
+        quant(xg_codes[:], xg_scales[:], xg_bf[:])
+        quant(c_codes[:], c_scales[:], c_bf[:])
+        accs = [psum.tile([P, S], F32, name=f"acc{n}", tag=f"acc{n}") for n in range(NB)]
+
+        def w_pass(n):
+            nc.tensor.matmul_mx(
+                out=accs[n][:],
+                lhsT=w4_t[:, 2 * P * n : 2 * P * (n + 1)].bitcast(E2M1X4),
+                lhsT_scale=w4_s[:, P * n : P * (n + 1)],
+                rhs=xg_codes[:].bitcast(E4M3X4),
+                rhs_scale=xg_scales[:],
+                start=True,
+                stop=False,
+            )
+
+        def u_pass(n, q, k):
+            nc.tensor.matmul_mx(
+                out=accs[n][:],
+                lhsT=u_codes[q][:, k : k + P].bitcast(E4M3X4),
+                lhsT_scale=u_scales[q][:, k : k + P],
+                rhs=c_codes[:].bitcast(E4M3X4),
+                rhs_scale=c_scales[:],
+                start=False,
+                stop=True,
+            )
+
+        def finish(n):
+            if DRAIN_ON[n] == "S":
+                nc.scalar.activation(res[n][:], accs[n][:], IDENTITY, bias=b_cols[:, n : n + 1])
+            else:
+                nc.vector.tensor_scalar(res[n][:], accs[n][:], b_cols[:, n : n + 1], None, ADD)
+            nc.sync.dma_start(out[n * P : (n + 1) * P, :], res[n][:])
+
+        for q, (u0, w) in enumerate(zip(U_STARTS, U_WIDTHS)):
+            cut = U_SCALAR[q]
+            if cut > 0:
+                lay("S", u_bf[q][:, 0:cut, :], u_raw[q][:, :, 0:cut])
+            if cut < w:
+                lay("V", u_bf[q][:, cut:w, :], u_raw[q][:, :, cut:w])
+            quant(u_codes[q][:], u_scales[q][:], u_bf[q][:])
+            for k in range(0, w, P):
+                n = (u0 + k) // P
+                w_pass(n)
+                u_pass(n, q, k)
+                finish(n)

@@ -19,13 +19,15 @@ P = 128
 PACK = 4
 K, L, M, T, S = 512, 512, 1024, 2048, 512
 NB = M // P
-U_WIDTHS = (512, 256, 256,)
-U_STARTS = (0, 512, 768,)
-U_SCALAR = (192, 128, 128,)
-C_SCALAR = 192
+HEADS = 8
+U_WIDTHS = (256, 256, 256, 256,)
+U_STARTS = (0, 256, 512, 768,)
+U_SCALAR = (128, 128, 64, 0,)
+C_SCALAR = 320
 G_CUTS = (0, 256, 512)
-XG_ON = "SV"
-DRAIN_ON = "VSSVSSVS"
+PAIR0_ON = "SS"
+PAIR1_ON = "SV"
+DRAIN_ON = "SVSSSSVV"
 
 FLOPS = 2 * M * S * (K + L)
 
@@ -43,28 +45,33 @@ def tile_list_hmix_bias_kernel(tc, xT, w4_words, w4_scales, c, u, wgt, b, offs, 
         u_raw = [keep.tile([P, PACK, w], F32, name=f"u_raw{q}") for q, w in enumerate(U_WIDTHS)]
         w4_t = keep.tile([P, 2 * M], U8, name="w4_t", align_bytes=64)
         w4_s = keep.tile([P, M], U8, name="w4_s", align_bytes=64)
+        w_rows = keep.tile([P, P], F32, name="w_rows")
         b_rows = keep.tile([P, P], F32, name="b_rows")
+        head_cols = keep.tile([P, S // P, P], F32, name="head_cols")
         b_cols = keep.tile([P, NB], F32, name="b_cols")
         ident = keep.tile([P, P], F32, name="ident")
         warm = keep.tile([P, 1], F32, name="warm")
+        zero = keep.tile([P, 1], F32, name="zero")
 
         xv = xT.rearrange("(p j) t -> p j t", j=PACK)
         cv = c.rearrange("(p j) s -> p j s", j=PACK)
         uv = u.rearrange("(p j) n -> p j n", j=PACK)
 
+        nc.gpsimd.memset(w_rows[32:64, :], 0.0)
+        nc.gpsimd.memset(w_rows[64:P, :], 0.0)
         nc.vector.memset(b_rows[:], 0.0)
+        nc.vector.memset(zero[:], 0.0)
         nc.vector.memset(w4_s[:].bitcast(I32), 0)
         make_identity(nc, ident[:])
-        nc.scalar.activation(warm[:], b_rows[:, 0:1], IDENTITY)
 
         nc.sync.dma_start(offsets[:], offs)
+        nc.sync.dma_start(w_rows[0:32, :], wgt.rearrange("(g i) (q m) -> g q i m", i=P // HEADS, m=P)[:, :, 0, :])
         nc.scalar.dma_start(b_rows[0:NB, :], b.rearrange("(t m) -> t m", m=P))
         for q in range(4):
             nc.scalar.dma_start(
                 w4_s[32 * q : 32 * q + 4, :].bitcast(I32), w4_scales[0, 4 * q : 4 * q + 4, :].bitcast(I32)
             )
         nc.sync.dma_start(planes[0][:], xv[:, 0, :])
-        nc.sync.dma_start(weights[:], wgt)
         nc.sync.dma_start(planes[1][:], xv[:, 1, :])
         nc.sync.dma_start(planes[2][:], xv[:, 2, :])
         nc.sync.dma_start(planes[3][:], xv[:, 3, :])
@@ -73,10 +80,22 @@ def tile_list_hmix_bias_kernel(tc, xT, w4_words, w4_scales, c, u, wgt, b, offs, 
         nc.sync.dma_start(w4_t[:], w4_words[0])
         nc.sync.dma_start(u_raw[1][:], uv[:, :, U_STARTS[1] : U_STARTS[1] + U_WIDTHS[1]])
         nc.sync.dma_start(u_raw[2][:], uv[:, :, U_STARTS[2] : U_STARTS[2] + U_WIDTHS[2]])
+        nc.sync.dma_start(u_raw[3][:], uv[:, :, U_STARTS[3] : U_STARTS[3] + U_WIDTHS[3]])
 
+        nc.scalar.activation(warm[:], zero[:], IDENTITY)
+        turned = psum.tile([P, P], F32, name="turned", tag="acc6")
+        nc.tensor.transpose(turned[:], w_rows[:], ident[:])
+        nc.vector.tensor_copy(
+            head_cols[:].rearrange("p q (g i) -> p q g i", g=HEADS),
+            turned[:, 0:32].rearrange("p (g q) -> p q g", g=HEADS).unsqueeze(3).to_broadcast([P, S // P, HEADS, P // HEADS]),
+        )
+        spread = psum.tile([P, S], F32, name="spread", tag="acc5")
+        for q in range(S // P):
+            nc.tensor.transpose(spread[:, q * P : (q + 1) * P], head_cols[:, q, :], ident[:])
+        nc.scalar.copy(weights[:], spread[:])
         b_ps = psum.tile([P, P], F32, name="b_ps", tag="acc7")
         nc.tensor.transpose(b_ps[:], b_rows[:], ident[:])
-        nc.vector.tensor_copy(b_cols[:], b_ps[:, 0:NB])
+        nc.scalar.copy(b_cols[:], b_ps[:, 0:NB])
 
         c_bf = keep.tile([P, S, PACK], BF16, name="c_bf", align_bytes=64)
         c_codes = keep.tile([P, S], U32, name="c_codes", align_bytes=64)
@@ -96,13 +115,15 @@ def tile_list_hmix_bias_kernel(tc, xT, w4_words, w4_scales, c, u, wgt, b, offs, 
         def quant(codes, scales, src):
             nc.vector.quantize_mx(out=codes.bitcast(E4M3X4), scales=scales, in_=src.rearrange("p w j -> p (w j)"))
 
-        for i in range(PACK):
+        for pair, pair_on in ((0, PAIR0_ON), (1, PAIR1_ON)):
+            both = slice(2 * pair, 2 * pair + 2)
+            for i in (2 * pair, 2 * pair + 1):
+                for h, (lo, hi) in enumerate(zip(G_CUTS, G_CUTS[1:])):
+                    nc.vector.tensor_tensor(
+                        g[h][:, i, :], planes[i][:].indirect(offsets[:, lo // 16 : hi // 16]), weights[:, lo:hi], MULT
+                    )
             for h, (lo, hi) in enumerate(zip(G_CUTS, G_CUTS[1:])):
-                nc.vector.tensor_tensor(
-                    g[h][:, i, :], planes[i][:].indirect(offsets[:, lo // 16 : hi // 16]), weights[:, lo:hi], MULT
-                )
-        for h, (lo, hi) in enumerate(zip(G_CUTS, G_CUTS[1:])):
-            lay(XG_ON[h], xg_bf[:, lo:hi, :], g[h][:])
+                lay(pair_on[h], xg_bf[:, lo:hi, both], g[h][:, both, :])
 
         lay("S", c_bf[:, 0:C_SCALAR, :], c_raw[:, :, 0:C_SCALAR])
         lay("V", c_bf[:, C_SCALAR:S, :], c_raw[:, :, C_SCALAR:S])

@@ -22,12 +22,12 @@ NB = M // P
 HEADS = 8
 U_WIDTHS = (256, 256, 256, 256,)
 U_STARTS = (0, 256, 512, 768,)
-U_SCALAR = (128, 128, 64, 0,)
-C_SCALAR = 320
-G_CUTS = (0, 256, 512)
-PAIR0_ON = "SS"
+U_SCALAR = (160, 64, 0, 64,)
+C_SCALAR = 192
+G_CUTS = (0, 384, 512)
+PAIR0_ON = "SV"
 PAIR1_ON = "SV"
-DRAIN_ON = "SVSSSSVV"
+DRAIN_ON = "SSSVSSVV"
 
 FLOPS = 2 * M * S * (K + L)
 
@@ -76,8 +76,8 @@ def tile_list_hmix_bias_kernel(tc, xT, w4_words, w4_scales, c, u, wgt, b, offs, 
         nc.sync.dma_start(planes[2][:], xv[:, 2, :])
         nc.sync.dma_start(planes[3][:], xv[:, 3, :])
         nc.sync.dma_start(c_raw[:], cv)
-        nc.sync.dma_start(u_raw[0][:], uv[:, :, U_STARTS[0] : U_STARTS[0] + U_WIDTHS[0]])
         nc.sync.dma_start(w4_t[:], w4_words[0])
+        nc.sync.dma_start(u_raw[0][:], uv[:, :, U_STARTS[0] : U_STARTS[0] + U_WIDTHS[0]])
         nc.sync.dma_start(u_raw[1][:], uv[:, :, U_STARTS[1] : U_STARTS[1] + U_WIDTHS[1]])
         nc.sync.dma_start(u_raw[2][:], uv[:, :, U_STARTS[2] : U_STARTS[2] + U_WIDTHS[2]])
         nc.sync.dma_start(u_raw[3][:], uv[:, :, U_STARTS[3] : U_STARTS[3] + U_WIDTHS[3]])
@@ -110,7 +110,9 @@ def tile_list_hmix_bias_kernel(tc, xT, w4_words, w4_scales, c, u, wgt, b, offs, 
         res = [keep.tile([P, S], F32, name=f"res{n}") for n in range(NB)]
 
         def lay(engine, dst, src):
-            (nc.scalar.copy if engine == "S" else nc.vector.tensor_copy)(dst, src.rearrange("p j w -> p w j"))
+            (nc.scalar.copy if engine == "S" else nc.vector.tensor_copy)(
+                dst.rearrange("p (r i) j -> p r j i", i=4), src.rearrange("p j (r i) -> p r j i", i=4)
+            )
 
         def quant(codes, scales, src):
             nc.vector.quantize_mx(out=codes.bitcast(E4M3X4), scales=scales, in_=src.rearrange("p w j -> p (w j)"))

@@ -20,14 +20,14 @@ PACK = 4
 K, L, M, T, S = 512, 512, 1024, 2048, 512
 NB = M // P
 HEADS = 8
-U_WIDTHS = (256, 256, 256, 256,)
-U_STARTS = (0, 256, 512, 768,)
-U_SCALAR = (160, 64, 0, 64,)
-C_SCALAR = 192
-G_CUTS = (0, 384, 512)
-PAIR0_ON = "SV"
-PAIR1_ON = "SV"
-DRAIN_ON = "SSSVSSVV"
+U_WIDTHS = (256, 256, 256, 128, 128,)
+U_STARTS = (0, 256, 512, 768, 896,)
+U_SCALAR = (0, 192, 64, 0, 64,)
+C_SCALAR = 256
+G_CUTS = (0, 320, 512)
+PAIR0_ON = "VV"
+PAIR1_ON = "VS"
+DRAIN_ON = "SSSVVVSV"
 
 FLOPS = 2 * M * S * (K + L)
 
@@ -43,7 +43,7 @@ def tile_list_hmix_bias_kernel(tc, xT, w4_words, w4_scales, c, u, wgt, b, offs, 
         planes = [keep.tile([P, T], F32, name=f"plane{i}") for i in range(PACK)]
         c_raw = keep.tile([P, PACK, S], F32, name="c_raw")
         u_raw = [keep.tile([P, PACK, w], F32, name=f"u_raw{q}") for q, w in enumerate(U_WIDTHS)]
-        w4_t = keep.tile([P, 2 * M], U8, name="w4_t", align_bytes=64)
+        w4_t = [keep.tile([P, M], U8, name=f"w4_t{h}", align_bytes=64) for h in range(2)]
         w4_s = keep.tile([P, M], U8, name="w4_s", align_bytes=64)
         w_rows = keep.tile([P, P], F32, name="w_rows")
         b_rows = keep.tile([P, P], F32, name="b_rows")
@@ -74,13 +74,15 @@ def tile_list_hmix_bias_kernel(tc, xT, w4_words, w4_scales, c, u, wgt, b, offs, 
         nc.sync.dma_start(planes[0][:], xv[:, 0, :])
         nc.sync.dma_start(planes[1][:], xv[:, 1, :])
         nc.sync.dma_start(planes[2][:], xv[:, 2, :])
+        nc.sync.dma_start(w4_t[0][:], w4_words[0, :, 0:M])
         nc.sync.dma_start(planes[3][:], xv[:, 3, :])
         nc.sync.dma_start(c_raw[:], cv)
-        nc.sync.dma_start(w4_t[:], w4_words[0])
         nc.sync.dma_start(u_raw[0][:], uv[:, :, U_STARTS[0] : U_STARTS[0] + U_WIDTHS[0]])
         nc.sync.dma_start(u_raw[1][:], uv[:, :, U_STARTS[1] : U_STARTS[1] + U_WIDTHS[1]])
         nc.sync.dma_start(u_raw[2][:], uv[:, :, U_STARTS[2] : U_STARTS[2] + U_WIDTHS[2]])
         nc.sync.dma_start(u_raw[3][:], uv[:, :, U_STARTS[3] : U_STARTS[3] + U_WIDTHS[3]])
+        nc.sync.dma_start(u_raw[4][:], uv[:, :, U_STARTS[4] : U_STARTS[4] + U_WIDTHS[4]])
+        nc.sync.dma_start(w4_t[1][:], w4_words[0, :, M : 2 * M])
 
         nc.scalar.activation(warm[:], zero[:], IDENTITY)
         turned = psum.tile([P, P], F32, name="turned", tag="acc6")
@@ -129,30 +131,31 @@ def tile_list_hmix_bias_kernel(tc, xT, w4_words, w4_scales, c, u, wgt, b, offs, 
 
         lay("S", c_bf[:, 0:C_SCALAR, :], c_raw[:, :, 0:C_SCALAR])
         lay("V", c_bf[:, C_SCALAR:S, :], c_raw[:, :, C_SCALAR:S])
-        quant(xg_codes[:], xg_scales[:], xg_bf[:])
         quant(c_codes[:], c_scales[:], c_bf[:])
+        quant(xg_codes[:], xg_scales[:], xg_bf[:])
         accs = [psum.tile([P, S], F32, name=f"acc{n}", tag=f"acc{n}") for n in range(NB)]
 
-        def w_pass(n):
+        def w_pass(n, start):
+            h, k = divmod(2 * P * n, M)
             nc.tensor.matmul_mx(
                 out=accs[n][:],
-                lhsT=w4_t[:, 2 * P * n : 2 * P * (n + 1)].bitcast(E2M1X4),
+                lhsT=w4_t[h][:, k : k + 2 * P].bitcast(E2M1X4),
                 lhsT_scale=w4_s[:, P * n : P * (n + 1)],
                 rhs=xg_codes[:].bitcast(E4M3X4),
                 rhs_scale=xg_scales[:],
-                start=True,
-                stop=False,
+                start=start,
+                stop=not start,
             )
 
-        def u_pass(n, q, k):
+        def u_pass(n, q, k, start):
             nc.tensor.matmul_mx(
                 out=accs[n][:],
                 lhsT=u_codes[q][:, k : k + P].bitcast(E4M3X4),
                 lhsT_scale=u_scales[q][:, k : k + P],
                 rhs=c_codes[:].bitcast(E4M3X4),
                 rhs_scale=c_scales[:],
-                start=False,
-                stop=True,
+                start=start,
+                stop=not start,
             )
 
         def finish(n):
@@ -171,6 +174,10 @@ def tile_list_hmix_bias_kernel(tc, xT, w4_words, w4_scales, c, u, wgt, b, offs, 
             quant(u_codes[q][:], u_scales[q][:], u_bf[q][:])
             for k in range(0, w, P):
                 n = (u0 + k) // P
-                w_pass(n)
-                u_pass(n, q, k)
+                if n < NB // 2:
+                    w_pass(n, True)
+                    u_pass(n, q, k, False)
+                else:
+                    u_pass(n, q, k, True)
+                    w_pass(n, False)
                 finish(n)

from contextlib import ExitStack

import concourse.mybir as mybir
from concourse.masks import make_identity

F32 = mybir.dt.float32
BF16 = mybir.dt.bfloat16
I32 = mybir.dt.int32
U32 = mybir.dt.uint32
U16 = mybir.dt.uint16
U8 = mybir.dt.uint8
E4M3X4 = mybir.dt.float8_e4m3fn_x4
E2M1X4 = mybir.dt.float4_e2m1fn_x4
MULT = mybir.AluOpType.mult
ADD = mybir.AluOpType.add
IDENTITY = mybir.ActivationFunctionType.Identity

P = 128
PACK = 4
K, L, M, T, S = 512, 512, 1024, 2048, 512
NB = M // P
HEADS = 8
U_WIDTHS = (256, 256, 256, 128, 128,)
U_STARTS = (0, 256, 512, 768, 896,)
U_SCALAR = (0, 192, 64, 0, 64,)
C_SCALAR = 256
G_CUTS = (0, 320, 512)
PAIR0_ON = "VV"
PAIR1_ON = "VS"
DRAIN_ON = "SSSVVVSV"

FLOPS = 2 * M * S * (K + L)


def tile_list_hmix_bias_kernel(tc, xT, w4_words, w4_scales, c, u, wgt, b, offs, out):
    nc = tc.nc
    with ExitStack() as ctx:
        keep = ctx.enter_context(tc.tile_pool(name="keep", bufs=1))
        psum = ctx.enter_context(tc.psum_pool(name="psum", bufs=1))

        offsets = keep.tile([P, S // 16], U16, name="offsets")
        weights = keep.tile([P, S], F32, name="weights")
        planes = [keep.tile([P, T], F32, name=f"plane{i}") for i in range(PACK)]
        c_raw = keep.tile([P, PACK, S], F32, name="c_raw")
        u_raw = [keep.tile([P, PACK, w], F32, name=f"u_raw{q}") for q, w in enumerate(U_WIDTHS)]
        w4_t = [keep.tile([P, M], U8, name=f"w4_t{h}", align_bytes=64) for h in range(2)]
        w4_s = keep.tile([P, M], U8, name="w4_s", align_bytes=64)
        w_rows = keep.tile([P, P], F32, name="w_rows")
        b_rows = keep.tile([P, P], F32, name="b_rows")
        head_cols = keep.tile([P, S // P, P], F32, name="head_cols")
        b_cols = keep.tile([P, NB], F32, name="b_cols")
        ident = keep.tile([P, P], F32, name="ident")
        warm = keep.tile([P, 1], F32, name="warm")
        zero = keep.tile([P, 1], F32, name="zero")

        xv = xT.rearrange("(p j) t -> p j t", j=PACK)
        cv = c.rearrange("(p j) s -> p j s", j=PACK)
        uv = u.rearrange("(p j) n -> p j n", j=PACK)

        nc.gpsimd.memset(w_rows[32:64, :], 0.0)
        nc.gpsimd.memset(w_rows[64:P, :], 0.0)
        nc.vector.memset(b_rows[:], 0.0)
        nc.vector.memset(zero[:], 0.0)
        nc.vector.memset(w4_s[:].bitcast(I32), 0)
        make_identity(nc, ident[:])

        nc.sync.dma_start(offsets[:], offs)
        nc.sync.dma_start(w_rows[0:32, :], wgt.rearrange("(g i) (q m) -> g q i m", i=P // HEADS, m=P)[:, :, 0, :])
        nc.scalar.dma_start(b_rows[0:NB, :], b.rearrange("(t m) -> t m", m=P))
        for q in range(4):
            nc.scalar.dma_start(
                w4_s[32 * q : 32 * q + 4, :].bitcast(I32), w4_scales[0, 4 * q : 4 * q + 4, :].bitcast(I32)
            )
        nc.sync.dma_start(planes[0][:], xv[:, 0, :])
        nc.sync.dma_start(planes[1][:], xv[:, 1, :])
        nc.sync.dma_start(planes[2][:], xv[:, 2, :])
        nc.sync.dma_start(w4_t[0][:], w4_words[0, :, 0:M])
        nc.sync.dma_start(planes[3][:], xv[:, 3, :])
        nc.sync.dma_start(c_raw[:], cv)
        nc.sync.dma_start(u_raw[0][:], uv[:, :, U_STARTS[0] : U_STARTS[0] + U_WIDTHS[0]])
        nc.sync.dma_start(u_raw[1][:], uv[:, :, U_STARTS[1] : U_STARTS[1] + U_WIDTHS[1]])
        nc.sync.dma_start(u_raw[2][:], uv[:, :, U_STARTS[2] : U_STARTS[2] + U_WIDTHS[2]])
        nc.sync.dma_start(u_raw[3][:], uv[:, :, U_STARTS[3] : U_STARTS[3] + U_WIDTHS[3]])
        nc.sync.dma_start(u_raw[4][:], uv[:, :, U_STARTS[4] : U_STARTS[4] + U_WIDTHS[4]])
        nc.sync.dma_start(w4_t[1][:], w4_words[0, :, M : 2 * M])

        nc.scalar.activation(warm[:], zero[:], IDENTITY)
        turned = psum.tile([P, P], F32, name="turned", tag="acc6")
        nc.tensor.transpose(turned[:], w_rows[:], ident[:])
        nc.vector.tensor_copy(
            head_cols[:].rearrange("p q (g i) -> p q g i", g=HEADS),
            turned[:, 0:32].rearrange("p (g q) -> p q g", g=HEADS).unsqueeze(3).to_broadcast([P, S // P, HEADS, P // HEADS]),
        )
        spread = psum.tile([P, S], F32, name="spread", tag="acc5")
        for q in range(S // P):
            nc.tensor.transpose(spread[:, q * P : (q + 1) * P], head_cols[:, q, :], ident[:])
        nc.scalar.copy(weights[:], spread[:])
        b_ps = psum.tile([P, P], F32, name="b_ps", tag="acc7")
        nc.tensor.transpose(b_ps[:], b_rows[:], ident[:])
        nc.scalar.copy(b_cols[:], b_ps[:, 0:NB])

        c_bf = keep.tile([P, S, PACK], BF16, name="c_bf", align_bytes=64)
        c_codes = keep.tile([P, S], U32, name="c_codes", align_bytes=64)
        c_scales = keep.tile([P, S], U8, name="c_scales", align_bytes=64)
        g = [keep.tile([P, PACK, hi - lo], F32, name=f"g{lo}") for lo, hi in zip(G_CUTS, G_CUTS[1:])]
        u_bf = [keep.tile([P, w, PACK], BF16, name=f"u_bf{q}", align_bytes=64) for q, w in enumerate(U_WIDTHS)]
        u_codes = [keep.tile([P, w], U32, name=f"u_codes{q}", align_bytes=64) for q, w in enumerate(U_WIDTHS)]
        u_scales = [keep.tile([P, w], U8, name=f"u_scales{q}", align_bytes=64) for q, w in enumerate(U_WIDTHS)]
        xg_bf = keep.tile([P, S, PACK], BF16, name="xg_bf", align_bytes=64)
        xg_codes = keep.tile([P, S], U32, name="xg_codes", align_bytes=64)
        xg_scales = keep.tile([P, S], U8, name="xg_scales", align_bytes=64)
        res = [keep.tile([P, S], F32, name=f"res{n}") for n in range(NB)]

        def lay(engine, dst, src):
            (nc.scalar.copy if engine == "S" else nc.vector.tensor_copy)(
                dst.rearrange("p (r i) j -> p r j i", i=4), src.rearrange("p j (r i) -> p r j i", i=4)
            )

        def quant(codes, scales, src):
            nc.vector.quantize_mx(out=codes.bitcast(E4M3X4), scales=scales, in_=src.rearrange("p w j -> p (w j)"))

        for pair, pair_on in ((0, PAIR0_ON), (1, PAIR1_ON)):
            both = slice(2 * pair, 2 * pair + 2)
            for i in (2 * pair, 2 * pair + 1):
                for h, (lo, hi) in enumerate(zip(G_CUTS, G_CUTS[1:])):
                    nc.vector.tensor_tensor(
                        g[h][:, i, :], planes[i][:].indirect(offsets[:, lo // 16 : hi // 16]), weights[:, lo:hi], MULT
                    )
            for h, (lo, hi) in enumerate(zip(G_CUTS, G_CUTS[1:])):
                lay(pair_on[h], xg_bf[:, lo:hi, both], g[h][:, both, :])

        lay("S", c_bf[:, 0:C_SCALAR, :], c_raw[:, :, 0:C_SCALAR])
        lay("V", c_bf[:, C_SCALAR:S, :], c_raw[:, :, C_SCALAR:S])
        quant(c_codes[:], c_scales[:], c_bf[:])
        quant(xg_codes[:], xg_scales[:], xg_bf[:])
        accs = [psum.tile([P, S], F32, name=f"acc{n}", tag=f"acc{n}") for n in range(NB)]

        def w_pass(n, start):
            h, k = divmod(2 * P * n, M)
            nc.tensor.matmul_mx(
                out=accs[n][:],
                lhsT=w4_t[h][:, k : k + 2 * P].bitcast(E2M1X4),
                lhsT_scale=w4_s[:, P * n : P * (n + 1)],
                rhs=xg_codes[:].bitcast(E4M3X4),
                rhs_scale=xg_scales[:],
                start=start,
                stop=not start,
            )

        def u_pass(n, q, k, start):
            nc.tensor.matmul_mx(
                out=accs[n][:],
                lhsT=u_codes[q][:, k : k + P].bitcast(E4M3X4),
                lhsT_scale=u_scales[q][:, k : k + P],
                rhs=c_codes[:].bitcast(E4M3X4),
                rhs_scale=c_scales[:],
                start=start,
                stop=not start,
            )

        def finish(n):
            if DRAIN_ON[n] == "S":
                nc.scalar.activation(res[n][:], accs[n][:], IDENTITY, bias=b_cols[:, n : n + 1])
            else:
                nc.vector.tensor_scalar(res[n][:], accs[n][:], b_cols[:, n : n + 1], None, ADD)
            nc.sync.dma_start(out[n * P : (n + 1) * P, :], res[n][:])

        for q, (u0, w) in enumerate(zip(U_STARTS, U_WIDTHS)):
            cut = U_SCALAR[q]
            if cut > 0:
                lay("S", u_bf[q][:, 0:cut, :], u_raw[q][:, :, 0:cut])
            if cut < w:
                lay("V", u_bf[q][:, cut:w, :], u_raw[q][:, :, cut:w])
            quant(u_codes[q][:], u_scales[q][:], u_bf[q][:])
            for k in range(0, w, P):
                n = (u0 + k) // P
                if n < NB // 2:
                    w_pass(n, True)
                    u_pass(n, q, k, False)
                else:
                    u_pass(n, q, k, True)
                    w_pass(n, False)
                finish(n)
